import numpy as np
import ml_dtypes


def mxq(x, axis, fmt="e4m3"):
    dtype, down = {"e4m3": (ml_dtypes.float8_e4m3fn, 7), "e5m2": (ml_dtypes.float8_e5m2, 14)}[fmt]
    v = np.moveaxis(np.asarray(x, np.float32).astype(ml_dtypes.bfloat16).astype(np.float64), axis, -1)
    blocks = v.reshape(v.shape[:-1] + (-1, 32))
    amax = np.abs(blocks).max(-1, keepdims=True)
    byte = np.maximum(np.where(amax > 0, np.frexp(amax)[1] - 1 + 127, 0) - down, 1)
    scale = np.exp2(byte - 127.0)
    codes = (blocks / scale).astype(np.float32).astype(dtype).astype(np.float64)
    return np.moveaxis((codes * scale).reshape(v.shape), -1, axis)


WIDE = False


def mx_kscale(k):
    if not WIDE:
        return np.ones(k)
    levels = np.array([10, -10, 5, -5, 0])
    if k % 512:
        return np.exp2(np.random.permutation(np.resize(levels, k // 32))).repeat(32)
    a = np.empty((k // 512, 16))
    for p in range(k // 512):
        a[p, :8] = np.random.permutation(np.resize(levels, 8))
        for g in range(8):
            far = levels[np.abs(levels - a[p, g]) >= 10]
            a[p, g + 8] = far[np.random.randint(len(far))]
    return np.exp2(a.ravel()).repeat(32)


def f64(x):
    return np.asarray(x).astype(np.float64)


def striped(idx):
    return np.tile(idx.reshape(-1, 16).T, (8, 1)).astype(np.uint16)


def unstriped(offs):
    return offs[:16].T.reshape(-1).astype(np.int64)


def pack_weight(w):
    k, n = w.shape
    w = f64(np.asarray(w, np.float32).astype(ml_dtypes.bfloat16)).reshape(k // 32, 32, n)
    amax = np.abs(w).max(1)
    byte = np.clip(np.where(amax > 0, np.frexp(amax)[1] - 1 + 127 - 7, 1), 1, 254)
    scaled = (w * np.exp2(127.0 - byte)[:, None, :]).reshape(k, n).astype(np.float32)
    words = np.ascontiguousarray(scaled.reshape(k // 512, 128, 4, n).transpose(0, 1, 3, 2)).astype(ml_dtypes.float8_e4m3fn).view(np.uint8)
    return words, np.ascontiguousarray(byte.astype(np.uint8).reshape(k // 512, 16, n))


def unpack_weight(words, scales):
    g, p, n, _ = words.shape
    vals = np.ascontiguousarray(words).view(ml_dtypes.float8_e4m3fn).astype(np.float64) * np.repeat(np.exp2(scales.astype(np.float64) - 127.0), 8, axis=1)[..., None]
    return vals.transpose(0, 1, 3, 2).reshape(g * 512, n)


K, T, S, N, U = 512, 2048, 512, 256, 1024


def setup_inputs():
    n = np.random.standard_normal
    s = mx_kscale(K)[:, None]
    packed_xT = pack_weight(n((K, T)) * s)
    return {
        "x_words": packed_xT[0],
        "x_scales": packed_xT[1],
        "state": (n((N, U))).astype(np.float32),
        "w1": (n((K, N)) / np.sqrt(K) / s).astype(np.float32),
        "w2": (n((K, N)) / np.sqrt(K) / s).astype(np.float32),
        "bias": (-np.random.uniform(0.5, 2.0, (N, 1))).astype(np.float32),
        "rate": (-np.random.uniform(0.3, 2.0, (N, 1))).astype(np.float32),
        "offs": striped(np.random.permutation(T)[:S]),
        "slot": striped(np.random.permutation(U)[:S]),
    }


def reference(x_words, x_scales, state, w1, w2, bias, rate, offs, slot):
    old = f64(state)[:, unstriped(slot)]
    xq = unpack_weight(x_words, x_scales)[:, unstriped(offs)]
    dt = np.log(np.exp((mxq(f64(w1), 0, "e4m3").T @ xq) + f64(bias)) + 1.0)
    a = np.exp(f64(rate) * dt)
    y = mxq(f64(w2), 0, "e4m3").T @ xq
    new = old * a + dt * y
    out = f64(state).copy()
    out[:, unstriped(slot)] = new
    return out

from contextlib import ExitStack

import concourse.mybir as mybir

K, T, S, N, U = 512, 2048, 512, 256, 1024
FLOPS = 2 * 2 * K * N * S

F32 = mybir.dt.float32
BF16 = mybir.dt.bfloat16
I32 = mybir.dt.int32
U32 = mybir.dt.uint32
U16 = mybir.dt.uint16
U8 = mybir.dt.uint8
FP8X4 = mybir.dt.float8_e4m3fn_x4
ALU = mybir.AluOpType
ACT = mybir.ActivationFunctionType

P = 128
PACK = 4
BLOCKS = N // P
HALVES = 2
H = S // HALVES
EXP_CAP = 2.0**60


def tile_picked_ymamba_step_p_kernel(
    tc, x_words, x_scales, state, w1, w2, bias, rate, offs, slot, out
):
    nc = tc.nc
    with ExitStack() as ctx:
        keep = ctx.enter_context(tc.tile_pool(name="keep", bufs=1))
        psum = ctx.enter_context(tc.psum_pool(name="psum", bufs=1))

        offs_t = keep.tile([P, S // 16], U16, name="offs_t")
        slot_t = keep.tile([P, S // 16], U16, name="slot_t")
        xw = keep.tile([P, T], I32, name="xw", align_bytes=64)
        xs = keep.tile([P, T], U8, name="xs", align_bytes=64)
        w_raw = [keep.tile([P, PACK, N], F32, name=f"w_raw{i}", align_bytes=64) for i in range(2)]
        st = [keep.tile([P, U], F32, name=f"st{b}", align_bytes=64) for b in range(BLOCKS)]
        bias_t = keep.tile([P, BLOCKS, 1], F32, name="bias_t")
        rate_t = keep.tile([P, BLOCKS, 1], F32, name="rate_t")

        nc.vector.memset(xs[:].bitcast(I32), 0)
        nc.sync.dma_start(offs_t[:], offs)
        nc.sync.dma_start(w_raw[0][:], w1.rearrange("(p j) n -> p j n", j=PACK))
        for r in range(4):
            nc.sync.dma_start(xs[r:P:32, :].bitcast(I32), x_scales[0, r:16:4, :].bitcast(I32))
        nc.sync.dma_start(xw[:], x_words[0].rearrange("p n t -> p (n t)").bitcast(I32))
        with nc.allow_non_contiguous_dma(reason="one value a channel, one channel a partition"):
            nc.sync.dma_start(bias_t[:], bias.rearrange("(b p) o -> p b o", p=P))
        nc.sync.dma_start(w_raw[1][:], w2.rearrange("(p j) n -> p j n", j=PACK))
        nc.sync.dma_start(slot_t[:], slot)
        for b in range(BLOCKS):
            nc.sync.dma_start(st[b][:], state[b * P : (b + 1) * P, :])
        with nc.allow_non_contiguous_dma(reason="one value a channel, one channel a partition"):
            nc.sync.dma_start(rate_t[:], rate.rearrange("(b p) o -> p b o", p=P))

        w_bf = [keep.tile([P, N, PACK], BF16, name=f"w_bf{i}", align_bytes=64) for i in range(2)]
        w_codes = [keep.tile([P, N], U32, name=f"w_codes{i}", align_bytes=64) for i in range(2)]
        w_scales = [keep.tile([P, N], U8, name=f"w_scales{i}", align_bytes=64) for i in range(2)]

        def quantize(i):
            nc.vector.quantize_mx(
                out=w_codes[i][:].bitcast(FP8X4),
                scales=w_scales[i][:],
                in_=w_bf[i][:].rearrange("p n j -> p (n j)"),
            )

        def grouped_views(i):
            return (
                w_bf[i][:].rearrange("p (c r) j -> p c j r", r=4),
                w_raw[i][:].rearrange("p j (c r) -> p c j r", r=4),
            )

        gw = keep.tile([P, S], U32, name="gw", align_bytes=64)
        gs = keep.tile([P, S], U8, name="gs", align_bytes=64)

        nc.scalar.copy(*grouped_views(0))
        nc.vector.tensor_copy(gs[:], xs[:].indirect(offs_t[:]))
        quantize(0)

        def product(dst, i, b, cols):
            m = slice(b * P, (b + 1) * P)
            nc.tensor.matmul_mx(
                out=dst,
                lhsT=w_codes[i][:, m].bitcast(FP8X4),
                lhsT_scale=w_scales[i][:, m],
                rhs=gw[:, cols].bitcast(FP8X4),
                rhs_scale=gs[:, cols],
                start=True,
                stop=True,
            )

        z = [[psum.tile([P, H], F32, name=f"z{b}{h}") for h in range(HALVES)] for b in range(BLOCKS)]
        y = [psum.tile([P, S], F32, name=f"y{b}") for b in range(BLOCKS)]
        ez = keep.tile([P, BLOCKS, S], F32, name="ez")
        halves = [slice(h * H, (h + 1) * H) for h in range(HALVES)]
        half_offs = [slice(h * H // 16, (h + 1) * H // 16) for h in range(HALVES)]

        for h in range(HALVES):
            nc.vector.tensor_copy(gw[:, halves[h]], xw[:].bitcast(U32).indirect(offs_t[:, half_offs[h]]))
            for b in range(BLOCKS):
                product(z[b][h][:], 0, b, halves[h])
                nc.scalar.activation(ez[:, b, halves[h]], z[b][h][:], ACT.Exp, bias=bias_t[:, b, :])

        nc.vector.tensor_copy(*grouped_views(1))
        quantize(1)
        for b in range(BLOCKS):
            product(y[b][:], 1, b, slice(0, S))

        ez1 = keep.tile([P, BLOCKS, S], F32, name="ez1")
        nc.vector.tensor_scalar(ez1[:], ez[:], EXP_CAP, 1.0, ALU.min, ALU.add)
        ln = keep.tile([P, BLOCKS, S], F32, name="ln")
        for b in range(BLOCKS):
            nc.scalar.activation(ln[:, b, :], ez1[:, b, :], ACT.Ln)

        old = [keep.tile([P, S], F32, name=f"old{b}") for b in range(BLOCKS)]
        for b in range(BLOCKS):
            nc.vector.tensor_copy(old[b][:], st[b][:].indirect(slot_t[:]))

        dt = keep.tile([P, BLOCKS, S], F32, name="dt")
        dty = keep.tile([P, BLOCKS, S], F32, name="dty")
        for b in range(BLOCKS):
            for h in range(HALVES):
                nc.vector.scalar_tensor_tensor(
                    dt[:, b, halves[h]], z[b][h][:], bias_t[:, b, :], ln[:, b, halves[h]], ALU.add, ALU.max
                )
        for b in range(BLOCKS):
            nc.vector.tensor_tensor(dty[:, b, :], y[b][:], dt[:, b, :], ALU.mult)

        decay = keep.tile([P, BLOCKS, S], F32, name="decay")
        kept = keep.tile([P, BLOCKS, S], F32, name="kept")
        pieces = [(0, halves[0], half_offs[0]), (0, halves[1], half_offs[1]), (1, slice(0, S), slice(0, S // 16))]
        for b, cols, entries in pieces:
            nc.scalar.activation(decay[:, b, cols], dt[:, b, cols], ACT.Exp, scale=rate_t[:, b, :])

        def keep_old(b, cols, entries):
            nc.vector.tensor_tensor(kept[:, b, cols], old[b][:, cols], decay[:, b, cols], ALU.mult)

        def put(b, cols, entries):
            nc.vector.tensor_tensor(st[b][:].indirect(slot_t[:, entries]), kept[:, b, cols], dty[:, b, cols], ALU.add)

        keep_old(*pieces[0])
        keep_old(*pieces[1])
        put(*pieces[0])
        keep_old(*pieces[2])
        put(*pieces[1])
        nc.sync.dma_start(out[0:P, :], st[0][:])
        put(*pieces[2])
        nc.sync.dma_start(out[P : 2 * P, :], st[1][:])
